import numpy as np
import ml_dtypes


def mxq(x, axis, fmt="e4m3"):
    dtype, down = {"e4m3": (ml_dtypes.float8_e4m3fn, 7), "e5m2": (ml_dtypes.float8_e5m2, 14)}[fmt]
    v = np.moveaxis(np.asarray(x, np.float32).astype(ml_dtypes.bfloat16).astype(np.float64), axis, -1)
    blocks = v.reshape(v.shape[:-1] + (-1, 32))
    amax = np.abs(blocks).max(-1, keepdims=True)
    byte = np.maximum(np.where(amax > 0, np.frexp(amax)[1] - 1 + 127, 0) - down, 1)
    scale = np.exp2(byte - 127.0)
    codes = (blocks / scale).astype(np.float32).astype(dtype).astype(np.float64)
    return np.moveaxis((codes * scale).reshape(v.shape), -1, axis)


WIDE = False


def mx_kscale(k, group=512):
    if not WIDE:
        return np.ones(k)
    levels = np.array([10, -10, 5, -5, 0])
    if group != 512:
        return np.exp2(np.random.permutation(np.resize(levels, k // group))).repeat(group)
    if k % 512:
        return np.exp2(np.random.permutation(np.resize(levels, k // 32))).repeat(32)
    a = np.empty((k // 512, 16))
    for p in range(k // 512):
        a[p, :8] = np.random.permutation(np.resize(levels, 8))
        for g in range(8):
            far = levels[np.abs(levels - a[p, g]) >= 10]
            a[p, g + 8] = far[np.random.randint(len(far))]
    return np.exp2(a.ravel()).repeat(32)


def f64(x):
    return np.asarray(x).astype(np.float64)


def striped(idx):
    return np.tile(np.asarray(idx).reshape(-1, 16).T, (8, 1)).astype(np.uint16)


def unstriped(offs):
    return offs[:16].T.reshape(-1).astype(np.int64)


H, KV, D, NQ, N = 4, 4, 128, 512, 1024


def setup_inputs():
    n = np.random.standard_normal
    s = mx_kscale(D, 0)[:, None]
    u = mx_kscale(N)
    t = np.random.uniform(0.5, 2.0, N) * u
    v = n((KV, N, 128))
    return {
        "qT": (n((H, D, NQ)) * s * (0.70 / np.sqrt(D))).astype(np.float32),
        "kT": (n((KV, D, N)) / s).astype(np.float32),
        "t": t.reshape(N, 1).astype(np.float32),
        "v": (v / t[:, None]).astype(np.float32),
        "kb": (0.5 * n((N, 1))).astype(np.float32),
        "gn": np.tile(np.random.uniform(0.5, 2.0, 128), (128, 1)).astype(np.float32),
    }


def reference(qT, kT, t, v, kb, gn):
    a = mxq(f64(kT), 1, "e4m3").transpose(0, 2, 1) @ mxq(f64(qT), 1, "e4m3")
    a = a + f64(kb)
    p = np.maximum(a, 0.0)
    w = p * f64(t)
    y = mxq(w, 1, "e4m3").transpose(0, 2, 1) @ mxq(f64(v), 1, "e4m3")
    y = y / 16.0
    y = y / np.sqrt(np.mean(np.square(y), -1, keepdims=True) + 1e-5) * f64(gn)[:1]
    return y

@@ -1,0 +1,233 @@
+from contextlib import ExitStack
+
+import concourse.mybir as mybir
+
+H, D, NQ, N = 4, 128, 512, 1024
+FLOPS = 2 * 2 * H * NQ * N * D
+
+F32 = mybir.dt.float32
+BF16 = mybir.dt.bfloat16
+U32 = mybir.dt.uint32
+U8 = mybir.dt.uint8
+FP8X4 = mybir.dt.float8_e4m3fn_x4
+ACT = mybir.ActivationFunctionType
+ALU = mybir.AluOpType
+
+P = 128
+PACK = 4
+ROWS = D // PACK
+PASS = P * PACK
+PASSES = N // PASS
+TILE = 128
+VECTOR_SHARE = 84
+GROUP_STRIDE = 4
+UNIT_STRIDE = 3
+
+
+def tile_rows_a_relu_kb_onorm_kernel(tc, qT, kT, t, v, kb, gn, out):
+    nc = tc.nc
+    with ExitStack() as ctx:
+        sb = ctx.enter_context(tc.tile_pool(name="sb", bufs=1))
+        ps = ctx.enter_context(tc.psum_pool(name="ps", bufs=1))
+        ctx.enter_context(tc.manual_schedule())
+
+        def sbuf(name, shape, dtype):
+            return sb.tile(shape, dtype, name=name, align_bytes=64)
+
+        def quantised(name, words):
+            return sbuf(name + "_codes", [P, words], U32), sbuf(name + "_scales", [P, words], U8)
+
+        def quantise(dst, src, first, words):
+            codes, scales = dst
+            nc.vector.quantize_mx(
+                out=codes[:, first : first + words].bitcast(FP8X4),
+                scales=scales[:, first : first + words],
+                in_=src[:, PACK * first : PACK * (first + words)],
+            )
+
+        t_sb = sbuf("t_sb", [P, PASSES, PACK], F32)
+        kb_sb = sbuf("kb_sb", [P, PASSES, PACK], F32)
+        nc.scalar.dma_start(out=t_sb[:], in_=t.rearrange("(g p j) o -> p g (j o)", p=P, j=PACK))
+        nc.scalar.dma_start(out=kb_sb[:], in_=kb.rearrange("(g p j) o -> p g (j o)", p=P, j=PACK))
+
+        q_raw = sbuf("q_raw", [P, PACK, NQ], F32)
+        nc.sync.dma_start(out=q_raw[:], in_=qT.rearrange("h (p j) q -> (h p) j q", j=PACK))
+        k_rows = kT.rearrange("h (p j) n -> (h p) j n", j=PACK)
+        k_raw = []
+        for g in range(PASSES):
+            k_raw.append(sbuf("k_raw%d" % g, [P, PACK, PASS], F32))
+            nc.sync.dma_start(out=k_raw[g][:], in_=k_rows[:, :, g * PASS : (g + 1) * PASS])
+        v_raw = []
+        for h in range(H):
+            v_raw.append(sbuf("v_raw%d" % h, [P, PASSES, PACK * D], F32))
+            nc.sync.dma_start(out=v_raw[h][:], in_=v[h].rearrange("(g p j) e -> p g (j e)", p=P, j=PACK))
+        gn_sb = sbuf("gn_sb", [P, D], F32)
+        nc.sync.dma_start(out=gn_sb[:], in_=gn)
+
+        t_abs = sbuf("t_abs", [P, PASSES, PACK], F32)
+        t_sign = sbuf("t_sign", [P, PASSES, PACK], F32)
+        bias = sbuf("bias", [P, PASSES, PACK], F32)
+        nc.scalar.activation(out=t_abs[:], in_=t_sb[:], func=ACT.Abs)
+        nc.scalar.activation(out=t_sign[:], in_=t_sb[:], func=ACT.Sign)
+        nc.gpsimd.tensor_tensor(out=bias[:], in0=kb_sb[:], in1=t_abs[:], op=ALU.mult)
+
+        def deal(dst, raw, vector_share):
+            dst_v = dst[:].rearrange("p (x s j) -> p s j x", x=PACK, j=PACK)
+            src_v = raw[:].rearrange("p j (s x) -> p s j x", x=PACK)
+            nc.vector.tensor_copy(out=dst_v[:, :vector_share], in_=src_v[:, :vector_share])
+            if vector_share < TILE:
+                nc.scalar.copy(out=dst_v[:, vector_share:], in_=src_v[:, vector_share:])
+
+        q_bf = sbuf("q_bf", [P, PACK * NQ], BF16)
+        q_mx = quantised("q", NQ)
+        k_bf = [sbuf("k_bf%d" % g, [P, PACK * PASS], BF16) for g in range(PASSES)]
+        k_mx = [quantised("k%d" % g, PASS) for g in range(PASSES)]
+        v_bf = [sbuf("v_bf%d" % h, [P, PASSES * PACK * D], BF16) for h in range(H)]
+        v_mx = [quantised("v%d" % h, PASSES * D) for h in range(H)]
+
+        def pack_v(h, g):
+            width = PACK * D
+            nc.vector.tensor_tensor(
+                out=v_bf[h][:, g * width : (g + 1) * width].rearrange("p (c i j) -> p c j i", i=4, j=PACK),
+                in0=v_raw[h][:, g, :].rearrange("p (j c i) -> p c j i", i=4, j=PACK),
+                in1=t_sign[:, g, :].unsqueeze(1).unsqueeze(3).to_broadcast([P, D // 4, PACK, 4]),
+                op=ALU.mult,
+            )
+
+        deal(q_bf, q_raw, VECTOR_SHARE)
+        quantise(q_mx, q_bf, 0, NQ)
+        deal(k_bf[0], k_raw[0], VECTOR_SHARE)
+        quantise(k_mx[0], k_bf[0], 0, TILE)
+        quantise(k_mx[0], k_bf[0], TILE, TILE)
+        quantise(k_mx[0], k_bf[0], 2 * TILE, 2 * TILE)
+        deal(k_bf[1], k_raw[1], TILE)
+        pack_v(0, 0)
+        quantise(k_mx[1], k_bf[1], 0, PASS)
+        pack_v(0, 1)
+
+        groups = [(h, g) for g in range(PASSES) for h in range(H)]
+        units = sorted((GROUP_STRIDE * i + UNIT_STRIDE * r, i, r) for i in range(len(groups)) for r in range(PACK))
+        last_unit = {i: n for n, (key, i, r) in enumerate(units)}
+        banks_of = [2, 1, 1, 2]
+        score_banks = [
+            [ps.tile([P, NQ], F32, name="scores%d_%d" % (h, b)) for b in range(banks_of[h])] for h in range(H)
+        ]
+        y_banks = [ps.tile([P, PACK, D], F32, name="y%d" % b) for b in range(2)]
+        w_flat = [sbuf("w_flat%d" % i, [P, PACK, NQ], BF16) for i in range(len(groups))]
+        w_bf = [sbuf("w_bf%d" % i, [P, PACK * NQ], BF16) for i in range(len(groups))]
+        w_mx = [quantised("w%d" % i, NQ) for i in range(len(groups))]
+        squares = [sbuf("squares%d" % h, [P, PACK, D], BF16) for h in range(H)]
+        sums = [sbuf("sums%d" % h, [P, PACK], F32) for h in range(H)]
+        factor = [sbuf("factor%d" % h, [P, PACK], F32) for h in range(H)]
+        result = [sbuf("result%d" % h, [P, PACK, D], F32) for h in range(H)]
+
+        def weights(i, r):
+            h, g = groups[i]
+            bank = score_banks[h][r % banks_of[h]]
+            rows = slice(ROWS * h, ROWS * (h + 1))
+            tokens = slice(TILE * r, TILE * (r + 1))
+            for x in range(PACK):
+                queries = slice(TILE * x, TILE * (x + 1))
+                nc.tensor.matmul_mx(
+                    out=bank[:, queries],
+                    lhsT=k_mx[g][0][rows, tokens].bitcast(FP8X4),
+                    lhsT_scale=k_mx[g][1][rows, tokens],
+                    rhs=q_mx[0][rows, queries].bitcast(FP8X4),
+                    rhs_scale=q_mx[1][rows, queries],
+                    start=True,
+                    stop=True,
+                )
+            nc.scalar.activation(
+                out=w_flat[i][:, r, :],
+                in_=bank[:],
+                func=ACT.Relu,
+                scale=t_abs[:, g, r : r + 1],
+                bias=bias[:, g, r : r + 1],
+            )
+
+        def pack_w(i, vector_share):
+            dst_v = w_bf[i][:].rearrange("p (c i r) -> p c r i", i=4, r=PACK)
+            src_v = w_flat[i][:].rearrange("p r (c i) -> p c r i", i=4)
+            nc.vector.tensor_copy(out=dst_v[:, :vector_share], in_=src_v[:, :vector_share])
+            if vector_share < NQ // 4:
+                nc.scalar.copy(out=dst_v[:, vector_share:], in_=src_v[:, vector_share:])
+
+        def values(h, places):
+            for x in places:
+                queries = slice(TILE * x, TILE * (x + 1))
+                for g in range(PASSES):
+                    w_codes, w_scales = w_mx[groups.index((h, g))]
+                    features = slice(D * g, D * (g + 1))
+                    nc.tensor.matmul_mx(
+                        out=y_banks[h % 2][:, x, :],
+                        lhsT=w_codes[:, queries].bitcast(FP8X4),
+                        lhsT_scale=w_scales[:, queries],
+                        rhs=v_mx[h][0][:, features].bitcast(FP8X4),
+                        rhs_scale=v_mx[h][1][:, features],
+                        start=(g == 0),
+                        stop=(g == PASSES - 1),
+                    )
+
+        def sum_squares(h):
+            for x in range(PACK):
+                nc.scalar.activation(
+                    out=squares[h][:, x, :],
+                    in_=y_banks[h % 2][:, x, :],
+                    func=ACT.Square,
+                    scale=1.0 / 16.0,
+                    accum_out=sums[h][:, x : x + 1],
+                )
+
+        def root(h):
+            nc.scalar.activation(
+                out=factor[h][:], in_=sums[h][:], func=ACT.Abs_reciprocal_sqrt, scale=256.0 / D, bias=256.0 * 1e-5
+            )
+
+        def finish(h):
+            for x in range(PACK):
+                nc.vector.scalar_tensor_tensor(
+                    out=result[h][:, x, :],
+                    in0=y_banks[h % 2][:, x, :],
+                    scalar=factor[h][:, x : x + 1],
+                    in1=gn_sb[:],
+                    op0=ALU.mult,
+                    op1=ALU.mult,
+                )
+            nc.sync.dma_start(out=out[h].rearrange("(p x) e -> p x e", x=PACK), in_=result[h][:])
+
+        whole = NQ // 4
+        for n, (key, i, r) in enumerate(units):
+            weights(i, r)
+            if n == last_unit[H] + 5:
+                values(0, [0, 1])
+            if n == last_unit[H] + 6:
+                values(0, [2, 3])
+                sum_squares(0)
+            if n == last_unit[H] + 7:
+                root(0)
+            if n == last_unit[i] and i < len(groups) - 1:
+                pack_w(i, whole)
+                if i < H:
+                    quantise(v_mx[i], v_bf[i], 0, PASSES * D)
+                if i + 1 < H:
+                    pack_v(i + 1, 0)
+                if i == H + 2:
+                    finish(0)
+                quantise(w_mx[i], w_bf[i], 0, NQ)
+                if i + 1 < H:
+                    pack_v(i + 1, 1)
+        last = len(groups) - 1
+        values(1, range(PACK))
+        sum_squares(1)
+        root(1)
+        values(2, range(PACK))
+        pack_w(last, whole // 2)
+        finish(1)
+        quantise(w_mx[last], w_bf[last], 0, NQ)
+        sum_squares(2)
+        root(2)
+        values(3, range(PACK))
+        finish(2)
+        sum_squares(3)
+        root(3)
+        finish(3)

@@ -57,9 +57,8 @@ def tile_rows_a_relu_kb_onorm_kernel(tc, qT, kT, t, v, kb, gn, out):
         for g in range(PASSES):
             k_raw.append(sbuf("k_raw%d" % g, [P, PACK, PASS], F32))
             nc.sync.dma_start(out=k_raw[g][:], in_=k_rows[:, :, g * PASS : (g + 1) * PASS])
-        v_raw = []
-        for h in range(H):
-            v_raw.append(sbuf("v_raw%d" % h, [P, PASSES, PACK * D], F32))
+        v_raw = [sbuf("v_raw%d" % h, [P, PASSES, PACK * D], F32) for h in range(H)]
+        for h in (1, 2, 3, 0):
             nc.sync.dma_start(out=v_raw[h][:], in_=v[h].rearrange("(g p j) e -> p g (j e)", p=P, j=PACK))
         gn_sb = sbuf("gn_sb", [P, D], F32)
         nc.sync.dma_start(out=gn_sb[:], in_=gn)
@@ -67,6 +66,9 @@ def tile_rows_a_relu_kb_onorm_kernel(tc, qT, kT, t, v, kb, gn, out):
         t_abs = sbuf("t_abs", [P, PASSES, PACK], F32)
         t_sign = sbuf("t_sign", [P, PASSES, PACK], F32)
         bias = sbuf("bias", [P, PASSES, PACK], F32)
+        warm = sbuf("warm", [P, 2], F32)
+        nc.vector.memset(warm[:, 0:1], 1.0)
+        nc.scalar.activation(out=warm[:, 1:2], in_=warm[:, 0:1], func=ACT.Abs_reciprocal_sqrt)
         nc.scalar.activation(out=t_abs[:], in_=t_sb[:], func=ACT.Abs)
         nc.scalar.activation(out=t_sign[:], in_=t_sb[:], func=ACT.Sign)
         nc.gpsimd.tensor_tensor(out=bias[:], in0=kb_sb[:], in1=t_abs[:], op=ALU.mult)
@@ -101,18 +103,22 @@ def tile_rows_a_relu_kb_onorm_kernel(tc, qT, kT, t, v, kb, gn, out):
         quantise(k_mx[0], k_bf[0], TILE, TILE)
         quantise(k_mx[0], k_bf[0], 2 * TILE, 2 * TILE)
         deal(k_bf[1], k_raw[1], TILE)
-        pack_v(0, 0)
+        pack_v(1, 0)
         quantise(k_mx[1], k_bf[1], 0, PASS)
-        pack_v(0, 1)
+        pack_v(1, 1)
+        pack_v(2, 0)
+        quantise(v_mx[1], v_bf[1], 0, PASSES * D)
+        pack_v(2, 1)
 
-        groups = [(h, g) for g in range(PASSES) for h in range(H)]
+        groups = [(h, 0) for h in range(H)] + [((h + 1) % H, 1) for h in range(H)]
         units = sorted((GROUP_STRIDE * i + UNIT_STRIDE * r, i, r) for i in range(len(groups)) for r in range(PACK))
         last_unit = {i: n for n, (key, i, r) in enumerate(units)}
-        banks_of = [2, 1, 1, 2]
+        banks_of = [2, 1, 1, 1]
         score_banks = [
             [ps.tile([P, NQ], F32, name="scores%d_%d" % (h, b)) for b in range(banks_of[h])] for h in range(H)
         ]
-        y_banks = [ps.tile([P, PACK, D], F32, name="y%d" % b) for b in range(2)]
+        turn = [0] * H
+        y_banks = [ps.tile([P, PACK, D], F32, name="y%d" % b) for b in range(3)]
         w_flat = [sbuf("w_flat%d" % i, [P, PACK, NQ], BF16) for i in range(len(groups))]
         w_bf = [sbuf("w_bf%d" % i, [P, PACK * NQ], BF16) for i in range(len(groups))]
         w_mx = [quantised("w%d" % i, NQ) for i in range(len(groups))]
@@ -123,7 +129,8 @@ def tile_rows_a_relu_kb_onorm_kernel(tc, qT, kT, t, v, kb, gn, out):
 
         def weights(i, r):
             h, g = groups[i]
-            bank = score_banks[h][r % banks_of[h]]
+            bank = score_banks[h][turn[h] % banks_of[h]]
+            turn[h] = turn[h] + 1
             rows = slice(ROWS * h, ROWS * (h + 1))
             tokens = slice(TILE * r, TILE * (r + 1))
             for x in range(PACK):
@@ -145,21 +152,23 @@ def tile_rows_a_relu_kb_onorm_kernel(tc, qT, kT, t, v, kb, gn, out):
                 bias=bias[:, g, r : r + 1],
             )
 
-        def pack_w(i, vector_share):
+        def pack_w(engine, i, places):
+            cols = slice(places.start * TILE // 4, places.stop * TILE // 4)
             dst_v = w_bf[i][:].rearrange("p (c i r) -> p c r i", i=4, r=PACK)
             src_v = w_flat[i][:].rearrange("p r (c i) -> p c r i", i=4)
-            nc.vector.tensor_copy(out=dst_v[:, :vector_share], in_=src_v[:, :vector_share])
-            if vector_share < NQ // 4:
-                nc.scalar.copy(out=dst_v[:, vector_share:], in_=src_v[:, vector_share:])
+            engine(out=dst_v[:, cols], in_=src_v[:, cols])
 
-        def values(h, places):
+        def quantise_w(i, places):
+            quantise(w_mx[i], w_bf[i], places.start * TILE, len(places) * TILE)
+
+        def values(h, places, bank):
             for x in places:
                 queries = slice(TILE * x, TILE * (x + 1))
                 for g in range(PASSES):
                     w_codes, w_scales = w_mx[groups.index((h, g))]
                     features = slice(D * g, D * (g + 1))
                     nc.tensor.matmul_mx(
-                        out=y_banks[h % 2][:, x, :],
+                        out=y_banks[bank][:, x, :],
                         lhsT=w_codes[:, queries].bitcast(FP8X4),
                         lhsT_scale=w_scales[:, queries],
                         rhs=v_mx[h][0][:, features].bitcast(FP8X4),
@@ -168,66 +177,85 @@ def tile_rows_a_relu_kb_onorm_kernel(tc, qT, kT, t, v, kb, gn, out):
                         stop=(g == PASSES - 1),
                     )
 
-        def sum_squares(h):
-            for x in range(PACK):
+        def sum_squares(h, places, bank):
+            for x in places:
                 nc.scalar.activation(
                     out=squares[h][:, x, :],
-                    in_=y_banks[h % 2][:, x, :],
+                    in_=y_banks[bank][:, x, :],
                     func=ACT.Square,
                     scale=1.0 / 16.0,
                     accum_out=sums[h][:, x : x + 1],
                 )
 
-        def root(h):
+        def root(h, places):
+            cols = slice(places.start, places.stop)
             nc.scalar.activation(
-                out=factor[h][:], in_=sums[h][:], func=ACT.Abs_reciprocal_sqrt, scale=256.0 / D, bias=256.0 * 1e-5
+                out=factor[h][:, cols],
+                in_=sums[h][:, cols],
+                func=ACT.Abs_reciprocal_sqrt,
+                scale=256.0 / D,
+                bias=256.0 * 1e-5,
             )
 
-        def finish(h):
-            for x in range(PACK):
+        def finish(h, places, bank):
+            for x in places:
                 nc.vector.scalar_tensor_tensor(
                     out=result[h][:, x, :],
-                    in0=y_banks[h % 2][:, x, :],
+                    in0=y_banks[bank][:, x, :],
                     scalar=factor[h][:, x : x + 1],
                     in1=gn_sb[:],
                     op0=ALU.mult,
                     op1=ALU.mult,
                 )
-            nc.sync.dma_start(out=out[h].rearrange("(p x) e -> p x e", x=PACK), in_=result[h][:])
+            cols = slice(places.start, places.stop)
+            nc.sync.dma_start(out=out[h].rearrange("(p x) e -> p x e", x=PACK)[:, cols, :], in_=result[h][:, cols, :])
 
-        whole = NQ // 4
+        whole, front, back = range(PACK), range(PACK // 2), range(PACK // 2, PACK)
+        on_vector, on_scalar = nc.vector.tensor_copy, nc.scalar.copy
+        last = len(groups) - 1
         for n, (key, i, r) in enumerate(units):
             weights(i, r)
-            if n == last_unit[H] + 5:
-                values(0, [0, 1])
-            if n == last_unit[H] + 6:
-                values(0, [2, 3])
-                sum_squares(0)
-            if n == last_unit[H] + 7:
-                root(0)
-            if n == last_unit[i] and i < len(groups) - 1:
-                pack_w(i, whole)
-                if i < H:
-                    quantise(v_mx[i], v_bf[i], 0, PASSES * D)
-                if i + 1 < H:
-                    pack_v(i + 1, 0)
-                if i == H + 2:
-                    finish(0)
-                quantise(w_mx[i], w_bf[i], 0, NQ)
-                if i + 1 < H:
-                    pack_v(i + 1, 1)
-        last = len(groups) - 1
-        values(1, range(PACK))
-        sum_squares(1)
-        root(1)
-        values(2, range(PACK))
-        pack_w(last, whole // 2)
-        finish(1)
-        quantise(w_mx[last], w_bf[last], 0, NQ)
-        sum_squares(2)
-        root(2)
-        values(3, range(PACK))
-        finish(2)
-        sum_squares(3)
-        root(3)
-        finish(3)
+            if n == last_unit[i] and i < last - 1:
+                pack_w(on_vector, i, whole)
+                if i == 0:
+                    quantise(v_mx[2], v_bf[2], 0, PASSES * D)
+                if i in (1, 2):
+                    pack_v((i + 2) % H, 1)
+                if i == 3:
+                    quantise(v_mx[0], v_bf[0], 0, PASSES * D)
+                quantise_w(i, whole)
+                if i in (0, 1):
+                    pack_v((i + 3) % H, 0)
+                if i == 2:
+                    quantise(v_mx[3], v_bf[3], 0, PASSES * D)
+        pack_w(on_scalar, last, range(3, 4))
+        values(1, whole, 0)
+        values(2, whole, 1)
+        pack_w(on_vector, last - 1, whole)
+        sum_squares(1, whole, 0)
+        quantise_w(last - 1, whole)
+        values(3, whole, 2)
+        pack_w(on_vector, last, front)
+        sum_squares(2, range(0, 1), 1)
+        root(1, whole)
+        sum_squares(2, range(1, 4), 1)
+        finish(1, whole, 0)
+        quantise_w(last, front)
+        values(0, front, 0)
+        pack_w(on_vector, last, range(2, 3))
+        sum_squares(3, range(0, 1), 2)
+        root(2, whole)
+        sum_squares(3, range(1, 4), 2)
+        finish(2, whole, 1)
+        quantise_w(last, back)
+        values(0, back, 1)
+        sum_squares(0, range(0, 1), 0)
+        root(3, whole)
+        sum_squares(0, range(1, 2), 0)
+        finish(3, whole, 2)
+        sum_squares(0, range(2, 3), 1)
+        root(0, front)
+        sum_squares(0, range(3, 4), 1)
+        root(0, back)
+        finish(0, front, 0)
+        finish(0, back, 1)

@@ -19,9 +19,20 @@ ROWS = D // PACK
 PASS = P * PACK
 PASSES = N // PASS
 TILE = 128
-VECTOR_SHARE = 84
+RUN = 4
+Y_SCALE = 1.0 / 16.0
+EPS = 1e-5
+
+EVEN_SHARE = 84
+SMALL_SHARE = 44
+
 GROUP_STRIDE = 4
-UNIT_STRIDE = 3
+UNIT_STRIDE = 5
+REFILL = 3
+
+WHOLE = range(PACK)
+FRONT = range(PACK // 2)
+BACK = range(PACK // 2, PACK)
 
 
 def tile_rows_a_relu_kb_onorm_kernel(tc, qT, kT, t, v, kb, gn, out):
@@ -37,106 +48,110 @@ def tile_rows_a_relu_kb_onorm_kernel(tc, qT, kT, t, v, kb, gn, out):
         def quantised(name, words):
             return sbuf(name + "_codes", [P, words], U32), sbuf(name + "_scales", [P, words], U8)
 
-        def quantise(dst, src, first, words):
+        def quantise(dst, first, src):
             codes, scales = dst
-            nc.vector.quantize_mx(
-                out=codes[:, first : first + words].bitcast(FP8X4),
-                scales=scales[:, first : first + words],
-                in_=src[:, PACK * first : PACK * (first + words)],
-            )
+            cols = slice(first, first + src.shape[1] // PACK)
+            nc.vector.quantize_mx(out=codes[:, cols].bitcast(FP8X4), scales=scales[:, cols], in_=src)
+
+        groups = [(h, 0) for h in range(H)] + [((h - 1) % H, 1) for h in range(H)]
+        finishing = [h for h, g in groups[H:]]
 
         t_sb = sbuf("t_sb", [P, PASSES, PACK], F32)
         kb_sb = sbuf("kb_sb", [P, PASSES, PACK], F32)
-        nc.scalar.dma_start(out=t_sb[:], in_=t.rearrange("(g p j) o -> p g (j o)", p=P, j=PACK))
-        nc.scalar.dma_start(out=kb_sb[:], in_=kb.rearrange("(g p j) o -> p g (j o)", p=P, j=PACK))
+        nc.scalar.dma_start(out=t_sb[:], in_=t.rearrange("(g p r) o -> p g (r o)", p=P, r=PACK))
+        nc.scalar.dma_start(out=kb_sb[:], in_=kb.rearrange("(g p r) o -> p g (r o)", p=P, r=PACK))
 
         q_raw = sbuf("q_raw", [P, PACK, NQ], F32)
         nc.sync.dma_start(out=q_raw[:], in_=qT.rearrange("h (p j) q -> (h p) j q", j=PACK))
         k_rows = kT.rearrange("h (p j) n -> (h p) j n", j=PACK)
-        k_raw = []
+        k_raw = [sbuf("k_raw%d" % g, [P, PACK, PASS], F32) for g in range(PASSES)]
         for g in range(PASSES):
-            k_raw.append(sbuf("k_raw%d" % g, [P, PACK, PASS], F32))
             nc.sync.dma_start(out=k_raw[g][:], in_=k_rows[:, :, g * PASS : (g + 1) * PASS])
         v_raw = [sbuf("v_raw%d" % h, [P, PASSES, PACK * D], F32) for h in range(H)]
-        for h in (1, 2, 3, 0):
-            nc.sync.dma_start(out=v_raw[h][:], in_=v[h].rearrange("(g p j) e -> p g (j e)", p=P, j=PACK))
+        for h in finishing:
+            nc.sync.dma_start(out=v_raw[h][:], in_=v[h].rearrange("(g p r) e -> p g (r e)", p=P, r=PACK))
         gn_sb = sbuf("gn_sb", [P, D], F32)
         nc.sync.dma_start(out=gn_sb[:], in_=gn)
+
+        warm = sbuf("warm", [P, 2], F32)
+        nc.vector.memset(warm[:, 0:1], 1.0)
+        nc.scalar.activation(out=warm[:, 1:2], in_=warm[:, 0:1], func=ACT.Abs_reciprocal_sqrt)
 
         t_abs = sbuf("t_abs", [P, PASSES, PACK], F32)
         t_sign = sbuf("t_sign", [P, PASSES, PACK], F32)
         bias = sbuf("bias", [P, PASSES, PACK], F32)
-        warm = sbuf("warm", [P, 2], F32)
-        nc.vector.memset(warm[:, 0:1], 1.0)
-        nc.scalar.activation(out=warm[:, 1:2], in_=warm[:, 0:1], func=ACT.Abs_reciprocal_sqrt)
         nc.scalar.activation(out=t_abs[:], in_=t_sb[:], func=ACT.Abs)
         nc.scalar.activation(out=t_sign[:], in_=t_sb[:], func=ACT.Sign)
         nc.gpsimd.tensor_tensor(out=bias[:], in0=kb_sb[:], in1=t_abs[:], op=ALU.mult)
 
-        def deal(dst, raw, vector_share):
-            dst_v = dst[:].rearrange("p (x s j) -> p s j x", x=PACK, j=PACK)
-            src_v = raw[:].rearrange("p j (s x) -> p s j x", x=PACK)
-            nc.vector.tensor_copy(out=dst_v[:, :vector_share], in_=src_v[:, :vector_share])
+        def deal(name, raw, tiles, vector_share):
+            words = sbuf(name, [P, len(tiles) * TILE * PACK], BF16)
+            dst = words[:].rearrange("p (x s j) -> p s j x", x=len(tiles), j=PACK)
+            src = raw[:].rearrange("p j (s x) -> p s j x", x=PACK)[:, :, :, tiles.start : tiles.stop]
+            nc.vector.tensor_copy(out=dst[:, :vector_share], in_=src[:, :vector_share])
             if vector_share < TILE:
-                nc.scalar.copy(out=dst_v[:, vector_share:], in_=src_v[:, vector_share:])
+                nc.scalar.copy(out=dst[:, vector_share:], in_=src[:, vector_share:])
+            return words
 
-        q_bf = sbuf("q_bf", [P, PACK * NQ], BF16)
         q_mx = quantised("q", NQ)
-        k_bf = [sbuf("k_bf%d" % g, [P, PACK * PASS], BF16) for g in range(PASSES)]
         k_mx = [quantised("k%d" % g, PASS) for g in range(PASSES)]
-        v_bf = [sbuf("v_bf%d" % h, [P, PASSES * PACK * D], BF16) for h in range(H)]
         v_mx = [quantised("v%d" % h, PASSES * D) for h in range(H)]
+        v_words = [sbuf("v_bf%d" % h, [P, PASSES, D * PACK], BF16) for h in range(H)]
 
         def pack_v(h, g):
-            width = PACK * D
             nc.vector.tensor_tensor(
-                out=v_bf[h][:, g * width : (g + 1) * width].rearrange("p (c i j) -> p c j i", i=4, j=PACK),
-                in0=v_raw[h][:, g, :].rearrange("p (j c i) -> p c j i", i=4, j=PACK),
-                in1=t_sign[:, g, :].unsqueeze(1).unsqueeze(3).to_broadcast([P, D // 4, PACK, 4]),
+                out=v_words[h][:, g, :].rearrange("p (c i r) -> p c r i", i=RUN, r=PACK),
+                in0=v_raw[h][:, g, :].rearrange("p (r c i) -> p c r i", i=RUN, r=PACK),
+                in1=t_sign[:, g, :].unsqueeze(1).unsqueeze(3).to_broadcast([P, D // RUN, PACK, RUN]),
                 op=ALU.mult,
             )
 
-        deal(q_bf, q_raw, VECTOR_SHARE)
-        quantise(q_mx, q_bf, 0, NQ)
-        deal(k_bf[0], k_raw[0], VECTOR_SHARE)
-        quantise(k_mx[0], k_bf[0], 0, TILE)
-        quantise(k_mx[0], k_bf[0], TILE, TILE)
-        quantise(k_mx[0], k_bf[0], 2 * TILE, 2 * TILE)
-        deal(k_bf[1], k_raw[1], TILE)
-        pack_v(1, 0)
-        quantise(k_mx[1], k_bf[1], 0, PASS)
-        pack_v(1, 1)
-        pack_v(2, 0)
-        quantise(v_mx[1], v_bf[1], 0, PASSES * D)
-        pack_v(2, 1)
+        def quantise_v(h):
+            quantise(v_mx[h], 0, v_words[h][:].rearrange("p g w -> p (g w)"))
 
-        groups = [(h, 0) for h in range(H)] + [((h + 1) % H, 1) for h in range(H)]
-        units = sorted((GROUP_STRIDE * i + UNIT_STRIDE * r, i, r) for i in range(len(groups)) for r in range(PACK))
-        last_unit = {i: n for n, (key, i, r) in enumerate(units)}
-        banks_of = [2, 1, 1, 1]
-        score_banks = [
-            [ps.tile([P, NQ], F32, name="scores%d_%d" % (h, b)) for b in range(banks_of[h])] for h in range(H)
-        ]
-        turn = [0] * H
-        y_banks = [ps.tile([P, PACK, D], F32, name="y%d" % b) for b in range(3)]
-        w_flat = [sbuf("w_flat%d" % i, [P, PACK, NQ], BF16) for i in range(len(groups))]
-        w_bf = [sbuf("w_bf%d" % i, [P, PACK * NQ], BF16) for i in range(len(groups))]
+        quantise(q_mx, 0, deal("q_bf", q_raw, WHOLE, EVEN_SHARE)[:])
+        k_front = deal("k_front", k_raw[0], FRONT, EVEN_SHARE)
+        k_back = deal("k_back", k_raw[0], BACK, SMALL_SHARE)
+        quantise(k_mx[0], 0, k_front[:, : TILE * PACK])
+        quantise(k_mx[0], TILE, k_front[:, TILE * PACK :])
+        quantise(k_mx[0], 2 * TILE, k_back[:])
+        k_second = deal("k_second", k_raw[1], WHOLE, TILE)
+        pack_v(finishing[0], 0)
+        quantise(k_mx[1], 0, k_second[:])
+        pack_v(finishing[0], 1)
+        for before, h in zip(finishing, finishing[1:]):
+            pack_v(h, 0)
+            quantise_v(before)
+            pack_v(h, 1)
+        quantise_v(finishing[-1])
+
+        head_bank = [ps.tile([P, NQ], F32, name="scores%d" % h) for h in range(H)]
+        spare_bank = ps.tile([P, NQ], F32, name="scores%d_second" % finishing[0])
+        score_bank = [spare_bank if i == H else head_bank[h] for i, (h, g) in enumerate(groups)]
+        bank_name = [H if i == H else h for i, (h, g) in enumerate(groups)]
+        y_bank = [ps.tile([P, PACK, D], F32, name="y%d" % b) for b in range(H - 1)]
+
+        waiting = sorted((GROUP_STRIDE * i + UNIT_STRIDE * r, i, r) for i in range(len(groups)) for r in WHOLE)
+        units = []
+        while waiting:
+            busy = [bank_name[i] for rank, i, r in units[-REFILL:]]
+            free = [unit for unit in waiting if bank_name[unit[1]] not in busy]
+            units.append((free or waiting)[0])
+            waiting.remove(units[-1])
+        last_unit = {i: n for n, (rank, i, r) in enumerate(units)}
+
+        w_rows = [sbuf("w_flat%d" % i, [P, PACK, NQ], BF16) for i in range(len(groups))]
+        w_words = [sbuf("w_bf%d" % i, [P, NQ * PACK], BF16) for i in range(len(groups))]
         w_mx = [quantised("w%d" % i, NQ) for i in range(len(groups))]
-        squares = [sbuf("squares%d" % h, [P, PACK, D], BF16) for h in range(H)]
-        sums = [sbuf("sums%d" % h, [P, PACK], F32) for h in range(H)]
-        factor = [sbuf("factor%d" % h, [P, PACK], F32) for h in range(H)]
-        result = [sbuf("result%d" % h, [P, PACK, D], F32) for h in range(H)]
 
         def weights(i, r):
             h, g = groups[i]
-            bank = score_banks[h][turn[h] % banks_of[h]]
-            turn[h] = turn[h] + 1
             rows = slice(ROWS * h, ROWS * (h + 1))
             tokens = slice(TILE * r, TILE * (r + 1))
-            for x in range(PACK):
+            for x in WHOLE:
                 queries = slice(TILE * x, TILE * (x + 1))
                 nc.tensor.matmul_mx(
-                    out=bank[:, queries],
+                    out=score_bank[i][:, queries],
                     lhsT=k_mx[g][0][rows, tokens].bitcast(FP8X4),
                     lhsT_scale=k_mx[g][1][rows, tokens],
                     rhs=q_mx[0][rows, queries].bitcast(FP8X4),
@@ -145,30 +160,41 @@ def tile_rows_a_relu_kb_onorm_kernel(tc, qT, kT, t, v, kb, gn, out):
                     stop=True,
                 )
             nc.scalar.activation(
-                out=w_flat[i][:, r, :],
-                in_=bank[:],
+                out=w_rows[i][:, r, :],
+                in_=score_bank[i][:],
                 func=ACT.Relu,
                 scale=t_abs[:, g, r : r + 1],
                 bias=bias[:, g, r : r + 1],
             )
 
-        def pack_w(engine, i, places):
-            cols = slice(places.start * TILE // 4, places.stop * TILE // 4)
-            dst_v = w_bf[i][:].rearrange("p (c i r) -> p c r i", i=4, r=PACK)
-            src_v = w_flat[i][:].rearrange("p r (c i) -> p c r i", i=4)
-            engine(out=dst_v[:, cols], in_=src_v[:, cols])
+        def pack_w(i, tiles):
+            runs = slice(tiles.start * TILE // RUN, tiles.stop * TILE // RUN)
+            dst = w_words[i][:].rearrange("p (c i r) -> p c r i", i=RUN, r=PACK)
+            src = w_rows[i][:].rearrange("p r (c i) -> p c r i", i=RUN)
+            nc.vector.tensor_copy(out=dst[:, runs], in_=src[:, runs])
 
-        def quantise_w(i, places):
-            quantise(w_mx[i], w_bf[i], places.start * TILE, len(places) * TILE)
+        def quantise_w(i, tiles):
+            quantise(w_mx[i], tiles.start * TILE, w_words[i][:, tiles.start * TILE * PACK : tiles.stop * TILE * PACK])
 
-        def values(h, places, bank):
-            for x in places:
+        def pack_and_quantise_w(i):
+            pack_w(i, FRONT)
+            pack_w(i, BACK)
+            quantise_w(i, FRONT)
+            quantise_w(i, BACK)
+
+        squares = [sbuf("squares%d" % h, [P, PACK, D], BF16) for h in range(H)]
+        sums = [sbuf("sums%d" % h, [P, PACK], F32) for h in range(H)]
+        factor = [sbuf("factor%d" % h, [P, PACK], F32) for h in range(H)]
+        result = [sbuf("result%d" % h, [P, PACK, D], F32) for h in range(H)]
+
+        def values(h, tiles, bank):
+            for x in tiles:
                 queries = slice(TILE * x, TILE * (x + 1))
                 for g in range(PASSES):
                     w_codes, w_scales = w_mx[groups.index((h, g))]
                     features = slice(D * g, D * (g + 1))
                     nc.tensor.matmul_mx(
-                        out=y_banks[bank][:, x, :],
+                        out=bank[:, x, :],
                         lhsT=w_codes[:, queries].bitcast(FP8X4),
                         lhsT_scale=w_scales[:, queries],
                         rhs=v_mx[h][0][:, features].bitcast(FP8X4),
@@ -177,85 +203,68 @@ def tile_rows_a_relu_kb_onorm_kernel(tc, qT, kT, t, v, kb, gn, out):
                         stop=(g == PASSES - 1),
                     )
 
-        def sum_squares(h, places, bank):
-            for x in places:
+        def sum_squares(h, tiles, bank):
+            for x in tiles:
                 nc.scalar.activation(
                     out=squares[h][:, x, :],
-                    in_=y_banks[bank][:, x, :],
+                    in_=bank[:, x, :],
                     func=ACT.Square,
-                    scale=1.0 / 16.0,
+                    scale=Y_SCALE,
                     accum_out=sums[h][:, x : x + 1],
                 )
 
-        def root(h, places):
-            cols = slice(places.start, places.stop)
+        def root(h, tiles):
+            cols = slice(tiles.start, tiles.stop)
             nc.scalar.activation(
                 out=factor[h][:, cols],
                 in_=sums[h][:, cols],
                 func=ACT.Abs_reciprocal_sqrt,
-                scale=256.0 / D,
-                bias=256.0 * 1e-5,
+                scale=1.0 / (Y_SCALE * Y_SCALE * D),
+                bias=EPS / (Y_SCALE * Y_SCALE),
             )
 
-        def finish(h, places, bank):
-            for x in places:
+        def finish(h, tiles, bank):
+            for x in tiles:
                 nc.vector.scalar_tensor_tensor(
                     out=result[h][:, x, :],
-                    in0=y_banks[bank][:, x, :],
+                    in0=bank[:, x, :],
                     scalar=factor[h][:, x : x + 1],
                     in1=gn_sb[:],
                     op0=ALU.mult,
                     op1=ALU.mult,
                 )
-            cols = slice(places.start, places.stop)
+            cols = slice(tiles.start, tiles.stop)
             nc.sync.dma_start(out=out[h].rearrange("(p x) e -> p x e", x=PACK)[:, cols, :], in_=result[h][:, cols, :])
 
-        whole, front, back = range(PACK), range(PACK // 2), range(PACK // 2, PACK)
-        on_vector, on_scalar = nc.vector.tensor_copy, nc.scalar.copy
-        last = len(groups) - 1
-        for n, (key, i, r) in enumerate(units):
+        first, second, third, last = finishing
+        last_group = len(groups) - 1
+        for n, (rank, i, r) in enumerate(units):
+            if n == len(units) - 1:
+                values(first, FRONT, y_bank[0])
             weights(i, r)
-            if n == last_unit[i] and i < last - 1:
-                pack_w(on_vector, i, whole)
-                if i == 0:
-                    quantise(v_mx[2], v_bf[2], 0, PASSES * D)
-                if i in (1, 2):
-                    pack_v((i + 2) % H, 1)
-                if i == 3:
-                    quantise(v_mx[0], v_bf[0], 0, PASSES * D)
-                quantise_w(i, whole)
-                if i in (0, 1):
-                    pack_v((i + 3) % H, 0)
-                if i == 2:
-                    quantise(v_mx[3], v_bf[3], 0, PASSES * D)
-        pack_w(on_scalar, last, range(3, 4))
-        values(1, whole, 0)
-        values(2, whole, 1)
-        pack_w(on_vector, last - 1, whole)
-        sum_squares(1, whole, 0)
-        quantise_w(last - 1, whole)
-        values(3, whole, 2)
-        pack_w(on_vector, last, front)
-        sum_squares(2, range(0, 1), 1)
-        root(1, whole)
-        sum_squares(2, range(1, 4), 1)
-        finish(1, whole, 0)
-        quantise_w(last, front)
-        values(0, front, 0)
-        pack_w(on_vector, last, range(2, 3))
-        sum_squares(3, range(0, 1), 2)
-        root(2, whole)
-        sum_squares(3, range(1, 4), 2)
-        finish(2, whole, 1)
-        quantise_w(last, back)
-        values(0, back, 1)
-        sum_squares(0, range(0, 1), 0)
-        root(3, whole)
-        sum_squares(0, range(1, 2), 0)
-        finish(3, whole, 2)
-        sum_squares(0, range(2, 3), 1)
-        root(0, front)
-        sum_squares(0, range(3, 4), 1)
-        root(0, back)
-        finish(0, front, 0)
-        finish(0, back, 1)
+            if n == last_unit[i] and i < last_group:
+                pack_and_quantise_w(i)
+
+        values(first, BACK, y_bank[0])
+        values(second, WHOLE, y_bank[1])
+        values(third, WHOLE, y_bank[2])
+        pack_w(last_group, WHOLE)
+        sum_squares(first, WHOLE, y_bank[0])
+        root(first, WHOLE)
+        finish(first, WHOLE, y_bank[0])
+        quantise_w(last_group, FRONT)
+        values(last, FRONT, y_bank[0])
+        sum_squares(second, WHOLE, y_bank[1])
+        root(second, WHOLE)
+        quantise_w(last_group, BACK)
+        finish(second, WHOLE, y_bank[1])
+        values(last, BACK, y_bank[1])
+        sum_squares(third, WHOLE, y_bank[2])
+        root(third, WHOLE)
+        sum_squares(last, FRONT, y_bank[0])
+        finish(third, WHOLE, y_bank[2])
+        root(last, FRONT)
+        sum_squares(last, BACK, y_bank[1])
+        finish(last, FRONT, y_bank[0])
+        root(last, BACK)
+        finish(last, BACK, y_bank[1])

from contextlib import ExitStack

import concourse.mybir as mybir

H, D, NQ, N = 4, 128, 512, 1024
FLOPS = 2 * 2 * H * NQ * N * D

F32 = mybir.dt.float32
BF16 = mybir.dt.bfloat16
U32 = mybir.dt.uint32
U8 = mybir.dt.uint8
FP8X4 = mybir.dt.float8_e4m3fn_x4
ACT = mybir.ActivationFunctionType
ALU = mybir.AluOpType

P = 128
PACK = 4
ROWS = D // PACK
PASS = P * PACK
PASSES = N // PASS
TILE = 128
RUN = 4
Y_SCALE = 1.0 / 16.0
EPS = 1e-5

EVEN_SHARE = 84
SMALL_SHARE = 44

GROUP_STRIDE = 4
UNIT_STRIDE = 5
REFILL = 3

WHOLE = range(PACK)
FRONT = range(PACK // 2)
BACK = range(PACK // 2, PACK)


def tile_rows_a_relu_kb_onorm_kernel(tc, qT, kT, t, v, kb, gn, out):
    nc = tc.nc
    with ExitStack() as ctx:
        sb = ctx.enter_context(tc.tile_pool(name="sb", bufs=1))
        ps = ctx.enter_context(tc.psum_pool(name="ps", bufs=1))
        ctx.enter_context(tc.manual_schedule())

        def sbuf(name, shape, dtype):
            return sb.tile(shape, dtype, name=name, align_bytes=64)

        def quantised(name, words):
            return sbuf(name + "_codes", [P, words], U32), sbuf(name + "_scales", [P, words], U8)

        def quantise(dst, first, src):
            codes, scales = dst
            cols = slice(first, first + src.shape[1] // PACK)
            nc.vector.quantize_mx(out=codes[:, cols].bitcast(FP8X4), scales=scales[:, cols], in_=src)

        groups = [(h, 0) for h in range(H)] + [((h - 1) % H, 1) for h in range(H)]
        finishing = [h for h, g in groups[H:]]

        t_sb = sbuf("t_sb", [P, PASSES, PACK], F32)
        kb_sb = sbuf("kb_sb", [P, PASSES, PACK], F32)
        nc.scalar.dma_start(out=t_sb[:], in_=t.rearrange("(g p r) o -> p g (r o)", p=P, r=PACK))
        nc.scalar.dma_start(out=kb_sb[:], in_=kb.rearrange("(g p r) o -> p g (r o)", p=P, r=PACK))

        q_raw = sbuf("q_raw", [P, PACK, NQ], F32)
        nc.sync.dma_start(out=q_raw[:], in_=qT.rearrange("h (p j) q -> (h p) j q", j=PACK))
        k_rows = kT.rearrange("h (p j) n -> (h p) j n", j=PACK)
        k_raw = [sbuf("k_raw%d" % g, [P, PACK, PASS], F32) for g in range(PASSES)]
        for g in range(PASSES):
            nc.sync.dma_start(out=k_raw[g][:], in_=k_rows[:, :, g * PASS : (g + 1) * PASS])
        v_raw = [sbuf("v_raw%d" % h, [P, PASSES, PACK * D], F32) for h in range(H)]
        for h in finishing:
            nc.sync.dma_start(out=v_raw[h][:], in_=v[h].rearrange("(g p r) e -> p g (r e)", p=P, r=PACK))
        gn_sb = sbuf("gn_sb", [P, D], F32)
        nc.sync.dma_start(out=gn_sb[:], in_=gn)

        warm = sbuf("warm", [P, 2], F32)
        nc.vector.memset(warm[:, 0:1], 1.0)
        nc.scalar.activation(out=warm[:, 1:2], in_=warm[:, 0:1], func=ACT.Abs_reciprocal_sqrt)

        t_abs = sbuf("t_abs", [P, PASSES, PACK], F32)
        t_sign = sbuf("t_sign", [P, PASSES, PACK], F32)
        bias = sbuf("bias", [P, PASSES, PACK], F32)
        nc.scalar.activation(out=t_abs[:], in_=t_sb[:], func=ACT.Abs)
        nc.scalar.activation(out=t_sign[:], in_=t_sb[:], func=ACT.Sign)
        nc.gpsimd.tensor_tensor(out=bias[:], in0=kb_sb[:], in1=t_abs[:], op=ALU.mult)

        def deal(name, raw, tiles, vector_share):
            words = sbuf(name, [P, len(tiles) * TILE * PACK], BF16)
            dst = words[:].rearrange("p (x s j) -> p s j x", x=len(tiles), j=PACK)
            src = raw[:].rearrange("p j (s x) -> p s j x", x=PACK)[:, :, :, tiles.start : tiles.stop]
            nc.vector.tensor_copy(out=dst[:, :vector_share], in_=src[:, :vector_share])
            if vector_share < TILE:
                nc.scalar.copy(out=dst[:, vector_share:], in_=src[:, vector_share:])
            return words

        q_mx = quantised("q", NQ)
        k_mx = [quantised("k%d" % g, PASS) for g in range(PASSES)]
        v_mx = [quantised("v%d" % h, PASSES * D) for h in range(H)]
        v_words = [sbuf("v_bf%d" % h, [P, PASSES, D * PACK], BF16) for h in range(H)]

        def pack_v(h, g):
            nc.vector.tensor_tensor(
                out=v_words[h][:, g, :].rearrange("p (c i r) -> p c r i", i=RUN, r=PACK),
                in0=v_raw[h][:, g, :].rearrange("p (r c i) -> p c r i", i=RUN, r=PACK),
                in1=t_sign[:, g, :].unsqueeze(1).unsqueeze(3).to_broadcast([P, D // RUN, PACK, RUN]),
                op=ALU.mult,
            )

        def quantise_v(h):
            quantise(v_mx[h], 0, v_words[h][:].rearrange("p g w -> p (g w)"))

        quantise(q_mx, 0, deal("q_bf", q_raw, WHOLE, EVEN_SHARE)[:])
        k_front = deal("k_front", k_raw[0], FRONT, EVEN_SHARE)
        k_back = deal("k_back", k_raw[0], BACK, SMALL_SHARE)
        quantise(k_mx[0], 0, k_front[:, : TILE * PACK])
        quantise(k_mx[0], TILE, k_front[:, TILE * PACK :])
        quantise(k_mx[0], 2 * TILE, k_back[:])
        k_second = deal("k_second", k_raw[1], WHOLE, TILE)
        pack_v(finishing[0], 0)
        quantise(k_mx[1], 0, k_second[:])
        pack_v(finishing[0], 1)
        for before, h in zip(finishing, finishing[1:]):
            pack_v(h, 0)
            quantise_v(before)
            pack_v(h, 1)
        quantise_v(finishing[-1])

        head_bank = [ps.tile([P, NQ], F32, name="scores%d" % h) for h in range(H)]
        spare_bank = ps.tile([P, NQ], F32, name="scores%d_second" % finishing[0])
        score_bank = [spare_bank if i == H else head_bank[h] for i, (h, g) in enumerate(groups)]
        bank_name = [H if i == H else h for i, (h, g) in enumerate(groups)]
        y_bank = [ps.tile([P, PACK, D], F32, name="y%d" % b) for b in range(H - 1)]

        waiting = sorted((GROUP_STRIDE * i + UNIT_STRIDE * r, i, r) for i in range(len(groups)) for r in WHOLE)
        units = []
        while waiting:
            busy = [bank_name[i] for rank, i, r in units[-REFILL:]]
            free = [unit for unit in waiting if bank_name[unit[1]] not in busy]
            units.append((free or waiting)[0])
            waiting.remove(units[-1])
        last_unit = {i: n for n, (rank, i, r) in enumerate(units)}

        w_rows = [sbuf("w_flat%d" % i, [P, PACK, NQ], BF16) for i in range(len(groups))]
        w_words = [sbuf("w_bf%d" % i, [P, NQ * PACK], BF16) for i in range(len(groups))]
        w_mx = [quantised("w%d" % i, NQ) for i in range(len(groups))]

        def weights(i, r):
            h, g = groups[i]
            rows = slice(ROWS * h, ROWS * (h + 1))
            tokens = slice(TILE * r, TILE * (r + 1))
            for x in WHOLE:
                queries = slice(TILE * x, TILE * (x + 1))
                nc.tensor.matmul_mx(
                    out=score_bank[i][:, queries],
                    lhsT=k_mx[g][0][rows, tokens].bitcast(FP8X4),
                    lhsT_scale=k_mx[g][1][rows, tokens],
                    rhs=q_mx[0][rows, queries].bitcast(FP8X4),
                    rhs_scale=q_mx[1][rows, queries],
                    start=True,
                    stop=True,
                )
            nc.scalar.activation(
                out=w_rows[i][:, r, :],
                in_=score_bank[i][:],
                func=ACT.Relu,
                scale=t_abs[:, g, r : r + 1],
                bias=bias[:, g, r : r + 1],
            )

        def pack_w(i, tiles):
            runs = slice(tiles.start * TILE // RUN, tiles.stop * TILE // RUN)
            dst = w_words[i][:].rearrange("p (c i r) -> p c r i", i=RUN, r=PACK)
            src = w_rows[i][:].rearrange("p r (c i) -> p c r i", i=RUN)
            nc.vector.tensor_copy(out=dst[:, runs], in_=src[:, runs])

        def quantise_w(i, tiles):
            quantise(w_mx[i], tiles.start * TILE, w_words[i][:, tiles.start * TILE * PACK : tiles.stop * TILE * PACK])

        def pack_and_quantise_w(i):
            pack_w(i, FRONT)
            pack_w(i, BACK)
            quantise_w(i, FRONT)
            quantise_w(i, BACK)

        squares = [sbuf("squares%d" % h, [P, PACK, D], BF16) for h in range(H)]
        sums = [sbuf("sums%d" % h, [P, PACK], F32) for h in range(H)]
        factor = [sbuf("factor%d" % h, [P, PACK], F32) for h in range(H)]
        result = [sbuf("result%d" % h, [P, PACK, D], F32) for h in range(H)]

        def values(h, tiles, bank):
            for x in tiles:
                queries = slice(TILE * x, TILE * (x + 1))
                for g in range(PASSES):
                    w_codes, w_scales = w_mx[groups.index((h, g))]
                    features = slice(D * g, D * (g + 1))
                    nc.tensor.matmul_mx(
                        out=bank[:, x, :],
                        lhsT=w_codes[:, queries].bitcast(FP8X4),
                        lhsT_scale=w_scales[:, queries],
                        rhs=v_mx[h][0][:, features].bitcast(FP8X4),
                        rhs_scale=v_mx[h][1][:, features],
                        start=(g == 0),
                        stop=(g == PASSES - 1),
                    )

        def sum_squares(h, tiles, bank):
            for x in tiles:
                nc.scalar.activation(
                    out=squares[h][:, x, :],
                    in_=bank[:, x, :],
                    func=ACT.Square,
                    scale=Y_SCALE,
                    accum_out=sums[h][:, x : x + 1],
                )

        def root(h, tiles):
            cols = slice(tiles.start, tiles.stop)
            nc.scalar.activation(
                out=factor[h][:, cols],
                in_=sums[h][:, cols],
                func=ACT.Abs_reciprocal_sqrt,
                scale=1.0 / (Y_SCALE * Y_SCALE * D),
                bias=EPS / (Y_SCALE * Y_SCALE),
            )

        def finish(h, tiles, bank):
            for x in tiles:
                nc.vector.scalar_tensor_tensor(
                    out=result[h][:, x, :],
                    in0=bank[:, x, :],
                    scalar=factor[h][:, x : x + 1],
                    in1=gn_sb[:],
                    op0=ALU.mult,
                    op1=ALU.mult,
                )
            cols = slice(tiles.start, tiles.stop)
            nc.sync.dma_start(out=out[h].rearrange("(p x) e -> p x e", x=PACK)[:, cols, :], in_=result[h][:, cols, :])

        first, second, third, last = finishing
        last_group = len(groups) - 1
        for n, (rank, i, r) in enumerate(units):
            if n == len(units) - 1:
                values(first, FRONT, y_bank[0])
            weights(i, r)
            if n == last_unit[i] and i < last_group:
                pack_and_quantise_w(i)

        values(first, BACK, y_bank[0])
        values(second, WHOLE, y_bank[1])
        values(third, WHOLE, y_bank[2])
        pack_w(last_group, WHOLE)
        sum_squares(first, WHOLE, y_bank[0])
        root(first, WHOLE)
        finish(first, WHOLE, y_bank[0])
        quantise_w(last_group, FRONT)
        values(last, FRONT, y_bank[0])
        sum_squares(second, WHOLE, y_bank[1])
        root(second, WHOLE)
        quantise_w(last_group, BACK)
        finish(second, WHOLE, y_bank[1])
        values(last, BACK, y_bank[1])
        sum_squares(third, WHOLE, y_bank[2])
        root(third, WHOLE)
        sum_squares(last, FRONT, y_bank[0])
        finish(third, WHOLE, y_bank[2])
        root(last, FRONT)
        sum_squares(last, BACK, y_bank[1])
        finish(last, FRONT, y_bank[0])
        root(last, BACK)
        finish(last, BACK, y_bank[1])
